import numpy as np
import ml_dtypes


def mxq(x, axis, fmt="e4m3"):
    dtype, down = {"e4m3": (ml_dtypes.float8_e4m3fn, 7), "e5m2": (ml_dtypes.float8_e5m2, 14)}[fmt]
    v = np.moveaxis(np.asarray(x, np.float32).astype(ml_dtypes.bfloat16).astype(np.float64), axis, -1)
    blocks = v.reshape(v.shape[:-1] + (-1, 32))
    amax = np.abs(blocks).max(-1, keepdims=True)
    byte = np.maximum(np.where(amax > 0, np.frexp(amax)[1] - 1 + 127, 0) - down, 1)
    scale = np.exp2(byte - 127.0)
    codes = (blocks / scale).astype(np.float32).astype(dtype).astype(np.float64)
    return np.moveaxis((codes * scale).reshape(v.shape), -1, axis)


WIDE = False


def mx_kscale(k):
    if not WIDE:
        return np.ones(k)
    levels = np.array([10, -10, 5, -5, 0])
    if k % 512:
        return np.exp2(np.random.permutation(np.resize(levels, k // 32))).repeat(32)
    a = np.empty((k // 512, 16))
    for p in range(k // 512):
        a[p, :8] = np.random.permutation(np.resize(levels, 8))
        for g in range(8):
            far = levels[np.abs(levels - a[p, g]) >= 10]
            a[p, g + 8] = far[np.random.randint(len(far))]
    return np.exp2(a.ravel()).repeat(32)


BF16 = ml_dtypes.bfloat16


def bf(x):
    return np.asarray(x, np.float32).astype(BF16)


def f64(x):
    return np.asarray(x).astype(np.float64)


E2M1 = np.array([0.0, 0.5, 1.0, 1.5, 2.0, 3.0, 4.0, 6.0, -0.0, -0.5, -1.0, -1.5, -2.0, -3.0, -4.0, -6.0])


def pack_weight(w, fmt):
    k, n = w.shape
    w = f64(bf(w)).reshape(k // 32, 32, n)
    amax = np.abs(w).max(1)
    if fmt == "e4m3":
        byte = np.frexp(amax)[1] - 1 + 127 - 7
    else:
        mant, ex = np.frexp(amax / 6.0)
        byte = np.where(mant > 0.5, ex, ex - 1) + 127
    byte = np.clip(np.where(amax > 0, byte, 1), 1, 254)
    scaled = (w * np.exp2(127.0 - byte)[:, None, :]).reshape(k, n).astype(np.float32)
    by_word = np.ascontiguousarray(scaled.reshape(k // 512, 128, 4, n).transpose(0, 1, 3, 2))
    if fmt == "e4m3":
        words = by_word.astype(ml_dtypes.float8_e4m3fn).view(np.uint8)
    else:
        c = by_word.astype(ml_dtypes.float4_e2m1fn).view(np.uint8) & 0xF
        words = c[..., 0::2] | (c[..., 1::2] << 4)
    return np.ascontiguousarray(words), np.ascontiguousarray(byte.astype(np.uint8).reshape(k // 512, 16, n))


def unpack_weight(words, scales, fmt):
    g, p, n, _ = words.shape
    if fmt == "e4m3":
        vals = np.ascontiguousarray(words).view(ml_dtypes.float8_e4m3fn).astype(np.float64)
    else:
        nib = np.empty((g, p, n, 4), np.uint8)
        nib[..., 0::2] = words & 0xF
        nib[..., 1::2] = words >> 4
        vals = E2M1[nib]
    vals = vals * np.repeat(np.exp2(scales.astype(np.float64) - 127.0), 8, axis=1)[..., None]
    return vals.transpose(0, 1, 3, 2).reshape(g * 512, n)
def pack4(w):
    words, scales = pack_weight(w, "e2m1")
    return words.reshape(words.shape[0], 128, -1), scales


def unpack4(words, scales):
    return unpack_weight(words.reshape(words.shape[0], 128, -1, 2), scales, "e2m1")


def planes(Y):
    n, m = Y.shape
    b = f64(bf(Y)).reshape(n // 32, 32, m)
    amax = np.abs(b).max(1)
    byte = np.clip(np.where(amax > 0, np.frexp(amax)[1] - 1 + 127 - 7, 1), 1, 254)
    codes = (b * np.exp2(127.0 - byte)[:, None, :]).reshape(n, m).astype(np.float32).astype(ml_dtypes.float8_e4m3fn).view(np.uint8)
    words = codes.reshape(n // 512, 128, 4, m).transpose(0, 1, 3, 2)
    return np.ascontiguousarray(words), np.ascontiguousarray(byte.astype(np.uint8).reshape(n // 512, 16, m))


NF, NL = 1024, 1024

SIZE_A = NL ** -0.25

def setup_inputs():
    rn = np.random.standard_normal
    s = mx_kscale(NF)
    v = mx_kscale(NL)
    u = mx_kscale(NL)
    F = rn((NF, NF)) * NF ** -0.5 * np.exp(0.3 * rn(NF))[None, :]
    f_words, f_scales = pack4(F * s[:, None])
    x = bf(rn((NF, NL)) * SIZE_A / s[:, None] * u[None, :])
    e = bf(0.5 * SIZE_A * rn((NF, NL)) * u[None, :])
    Z = rn((NL, NF)) * NL ** -0.5
    z_words, z_scales = pack_weight(Z * v[:, None], "e4m3")
    d = bf(rn((NL, NL)) * SIZE_A / v[:, None] / u[None, :])
    h = bf(0.5 * SIZE_A * rn(NL) / u)
    r = bf(rn((NF, NF)))
    penalty = bf(0.5 * np.exp(0.3 * rn(NF)))
    step = bf(np.exp(0.8 * rn(NF)))
    return {"f_words": f_words, "f_scales": f_scales, "x": x, "e": e, "z_words": z_words, "z_scales": z_scales,
            "d": d, "h": h, "r": r, "penalty": penalty, "step": step}

def reference(f_words, f_scales, x, e, z_words, z_scales, d, h, r, penalty, step):
    A = (unpack4(f_words, f_scales).T @ mxq(f64(x), 0, "e4m3")) + f64(e)
    B = (unpack_weight(z_words, z_scales, "e4m3").T @ mxq(f64(d), 0, "e4m3")) + f64(h)
    G = (mxq(A, 1, "e4m3") @ mxq(B, 1, "e4m3").T) + f64(penalty) * f64(r)
    y = G * f64(step)
    Y = y.T
    words, scales = planes(Y)
    return y, words, scales

@@ -1,0 +1,427 @@
+from contextlib import ExitStack
+
+import concourse.mybir as mybir
+from concourse.masks import make_identity
+
+F32 = mybir.dt.float32
+BF16 = mybir.dt.bfloat16
+U32 = mybir.dt.uint32
+I32 = mybir.dt.int32
+U8 = mybir.dt.uint8
+E4M3 = mybir.dt.float8_e4m3fn_x4
+E2M1 = mybir.dt.float4_e2m1fn_x4
+ADD = mybir.AluOpType.add
+MULT = mybir.AluOpType.mult
+COPY = mybir.ActivationFunctionType.Copy
+
+SIZE = 1024
+P = 128
+PACK = 4
+KP = P * PACK
+GROUPS = SIZE // KP
+AW = 256
+FLOPS = 3 * 2 * SIZE * SIZE * SIZE
+
+
+def tile_qap_reassignment_gradient_k4_kernel(
+    tc, f_words, f_scales, x, e, z_words, z_scales, d, h, r, penalty, step, out_0, out_1, out_2
+):
+    nc = tc.nc
+    with ExitStack() as ctx:
+        keep = ctx.enter_context(tc.tile_pool(name="keep", bufs=1))
+        work = ctx.enter_context(tc.tile_pool(name="work", bufs=1))
+        psum = ctx.enter_context(tc.psum_pool(name="psum", bufs=1))
+        ctx.enter_context(tc.manual_schedule())
+
+        t = {}
+
+        def kept(name, shape, dtype):
+            t[name] = keep.tile(shape, dtype, name=name, align_bytes=64)
+            return t[name]
+
+        def rotating(tag, name, shape, dtype, bufs):
+            t[name] = work.tile(shape, dtype, name=name, tag=tag, bufs=bufs, align_bytes=64)
+            return t[name]
+
+        def bank(name, index):
+            t[name] = psum.tile([P, KP], F32, name=name, tag="bank%d" % index)
+            return t[name]
+
+        def copy_on(engine, out, in_):
+            if engine is nc.scalar:
+                nc.scalar.copy(out=out, in_=in_)
+            else:
+                engine.tensor_copy(out=out, in_=in_)
+
+        def load_rows(name, src, kg, lg):
+            raw = kept("%s_raw%d%d" % (name, kg, lg), [P, PACK, KP], BF16)
+            rows = src[kg * KP : (kg + 1) * KP, lg * KP : (lg + 1) * KP]
+            nc.sync.dma_start(out=raw[:], in_=rows.rearrange("(p s) l -> p s l", s=PACK))
+
+        def load_tiles(name, src, q):
+            raw = kept("%s_raw%d" % (name, q), [P, AW // P, SIZE], BF16)
+            nc.sync.dma_start(out=raw[:], in_=src[q * AW : (q + 1) * AW, :].rearrange("(i p) n -> p i n", p=P))
+
+        def load_vector(name, src):
+            v = kept(name, [P, GROUPS, PACK], BF16)
+            nc.sync.dma_start(out=v[:], in_=src.rearrange("(g p t) -> p g t", p=P, t=PACK))
+
+        z_sc = kept("z_sc", [P, GROUPS, SIZE], U8)
+        f_sc = kept("f_sc", [P, GROUPS, SIZE], U8)
+        nc.vector.memset(z_sc[:].rearrange("p g n -> p (g n)").bitcast(I32), 0)
+        nc.vector.memset(f_sc[:].rearrange("p g n -> p (g n)").bitcast(I32), 0)
+
+        def load_scales(plane, src):
+            for quad in range(4):
+                nc.sync.dma_start(
+                    out=plane[32 * quad : 32 * quad + 4, :, :].bitcast(I32),
+                    in_=src[:, 4 * quad : 4 * quad + 4, :].rearrange("g r n -> r g n").bitcast(I32),
+                )
+
+        def load_z(g):
+            zc = kept("z_codes%d" % g, [P, GROUPS, KP], I32)
+            words = z_words[:, :, g * KP : (g + 1) * KP, :].rearrange("j p n t -> p j (n t)")
+            nc.sync.dma_start(out=zc[:], in_=words.bitcast(I32))
+
+        ident = kept("ident", [P, P], F32)
+        make_identity(nc, ident[:])
+
+        load_rows("d", d, 0, 0)
+        load_rows("d", d, 1, 0)
+        load_scales(z_sc, z_scales)
+        load_z(0)
+        load_rows("d", d, 0, 1)
+        load_vector("h", h)
+        load_rows("d", d, 1, 1)
+        load_z(1)
+        load_rows("x", x, 0, 0)
+        load_rows("x", x, 1, 0)
+        load_tiles("r", r, 0)
+        load_tiles("r", r, 1)
+        load_rows("x", x, 0, 1)
+        load_scales(f_sc, f_scales)
+        f_codes = kept("f_codes", [P, GROUPS, 2 * SIZE], U8)
+        nc.sync.dma_start(out=f_codes[:].bitcast(I32), in_=f_words.rearrange("g p n -> p g n").bitcast(I32))
+        load_rows("x", x, 1, 1)
+        load_vector("step", step)
+        load_vector("penalty", penalty)
+        load_tiles("e", e, 0)
+        load_tiles("e", e, 1)
+        load_tiles("r", r, 2)
+        load_tiles("r", r, 3)
+        load_tiles("e", e, 2)
+        load_tiles("e", e, 3)
+
+        def group_d(jg, lg, shares):
+            grp = rotating("grp", "d_grp%d%d" % (jg, lg), [P, PACK, P, PACK], BF16, 4)
+            raw = t["d_raw%d%d" % (jg, lg)][:].rearrange("p s (m t) -> p m s t", t=PACK)
+            for engine, slots in shares:
+                copy_on(engine, grp[:, slots].rearrange("p t m s -> p m s t"), raw[:, :, :, slots])
+
+        def group_x(bg, lg, engine):
+            grp = rotating("grp", "x_grp%d%d" % (bg, lg), [P, KP, PACK], BF16, 4)
+            copy_on(
+                engine,
+                grp[:].rearrange("p (c i) s -> p c s i", i=4),
+                t["x_raw%d%d" % (bg, lg)][:].rearrange("p s (c i) -> p c s i", i=4),
+            )
+
+        def quantize(codes, scales, values):
+            nc.vector.quantize_mx(out=codes.bitcast(E4M3), scales=scales, in_=values)
+
+        def quantize_input(name, kg, lg):
+            key = "%s_%s" + "%d%d" % (kg, lg)
+            codes = kept(key % (name, "codes"), [P, KP], U32)
+            scales = kept(key % (name, "sc"), [P, KP], U8)
+            grp = t[key % (name, "grp")]
+            flat = grp[:].rearrange("p t m s -> p (t m s)") if name == "d" else grp[:].rearrange("p c s -> p (c s)")
+            quantize(codes[:], scales[:], flat)
+
+        def b_matmuls(k, index):
+            lg, n = divmod(k, 8)
+            acc = bank("b_acc%d" % k, index)
+            cols = slice(n * P, (n + 1) * P)
+            for tl in range(PACK):
+                slot = slice(tl * P, (tl + 1) * P)
+                for jg in range(GROUPS):
+                    nc.tensor.matmul_mx(
+                        out=acc[:, slot],
+                        lhsT=t["d_codes%d%d" % (jg, lg)][:, slot].bitcast(E4M3),
+                        lhsT_scale=t["d_sc%d%d" % (jg, lg)][:, slot],
+                        rhs=t["z_codes%d" % (n // 4)][:, jg, n % 4 * P : (n % 4 + 1) * P].bitcast(E4M3),
+                        rhs_scale=z_sc[:, jg, cols],
+                        start=(jg == 0),
+                        stop=(jg == GROUPS - 1),
+                    )
+
+        def b_add(k):
+            lg, n = divmod(k, 8)
+            g, part = divmod(n, 4)
+            name = "b_grp%d%d" % (lg, g)
+            if part == 0:
+                rotating("b_grp", name, [P, PACK, P, PACK], BF16, 2)
+            nc.vector.tensor_tensor(
+                out=t[name][:, :, 32 * part : 32 * (part + 1), :],
+                in0=t["b_acc%d" % k][:].rearrange("p (tl m tc) -> p tc m tl", tl=PACK, tc=PACK),
+                in1=t["h"][:, lg, :].unsqueeze(1).unsqueeze(1).broadcast_to([P, PACK, 32, PACK]),
+                op=ADD,
+            )
+
+        def b_quantize(lg, g):
+            codes = kept("b_codes%d%d" % (lg, g), [P, KP], U32)
+            scales = kept("b_sc%d%d" % (lg, g), [P, KP], U8)
+            quantize(codes[:], scales[:], t["b_grp%d%d" % (lg, g)][:].rearrange("p t m s -> p (t m s)"))
+
+        def r_transposes(n, index):
+            half, g, u = r_units[n]
+            acc = bank("r_acc%d%d%d" % (half, g, u), index)
+            for i in range(4):
+                words = t["r_raw%d" % (2 * half + i // 2)][:, i % 2, :].bitcast(F32)
+                nc.tensor.transpose(acc[:, i * P : (i + 1) * P], words[:, 256 * g + u : 256 * (g + 1) : 2], ident[:])
+
+        def r_scale(n):
+            half, g, u = r_units[n]
+            pairs = t["r_acc%d%d%d" % (half, g, u)][:].bitcast(BF16).rearrange("p (a w) -> p a w", w=2)
+            for w in range(2):
+                tc_ = 2 * u + w
+                dst = kept("rps%d%d%d" % (half, g, tc_), [P, KP], F32)
+                nc.scalar.activation(out=dst[:], in_=pairs[:, :, w], func=COPY, scale=t["ps"][:, g, tc_ : tc_ + 1])
+
+        def a_matmuls(s, banks):
+            q, lg = a_steps[s]
+            for i in range(AW // P):
+                acc = bank("a_acc%d%d" % (s, i), banks[i])
+                a0 = q * AW + i * P
+                for bg in range(GROUPS):
+                    nc.tensor.matmul_mx(
+                        out=acc[:],
+                        lhsT=f_codes[:, bg, 2 * a0 : 2 * (a0 + P)].bitcast(E2M1),
+                        lhsT_scale=f_sc[:, bg, a0 : a0 + P],
+                        rhs=t["x_codes%d%d" % (bg, lg)][:].bitcast(E4M3),
+                        rhs_scale=t["x_sc%d%d" % (bg, lg)][:],
+                        start=(bg == 0),
+                        stop=(bg == GROUPS - 1),
+                    )
+
+        def a_add(s, i):
+            q, lg = a_steps[s]
+            dst = rotating("a_rows", "a_rows%d%d" % (s, i), [P, 2, P, 2], BF16, 6)
+            nc.vector.tensor_tensor(
+                out=dst[:],
+                in0=t["a_acc%d%d" % (s, i)][:].rearrange("a (p u w) -> a u p w", u=2, w=2),
+                in1=t["e_raw%d" % q][:, i, lg * KP : (lg + 1) * KP].rearrange("a (p u w) -> a u p w", u=2, w=2),
+                op=ADD,
+            )
+
+        def a_transposes(s, index):
+            acc = bank("a_turned%d" % s, index)
+            for i in range(AW // P):
+                words = t["a_rows%d%d" % (s, i)][:].rearrange("a u p w -> a (u p w)").bitcast(F32)
+                for u in range(2):
+                    col = u * AW + i * P
+                    nc.tensor.transpose(acc[:, col : col + P], words[:, u * P : (u + 1) * P], ident[:])
+
+        def a_copy(s):
+            grp = rotating("a_grp", "a_grp%d" % s, [P, AW * PACK], BF16, 2)
+            nc.scalar.copy(
+                out=grp[:].bitcast(F32).rearrange("p (a u) -> p a u", u=2),
+                in_=t["a_turned%d" % s][:].rearrange("p (u a) -> p a u", u=2),
+            )
+
+        def a_quantize(s):
+            codes = kept("a_codes%d" % s, [P, AW], U32)
+            scales = kept("a_sc%d" % s, [P, AW], U8)
+            quantize(codes[:], scales[:], t["a_grp%d" % s][:])
+
+        def g_matmuls(j, banks):
+            q, g = g_steps[j]
+            for u in range(2):
+                acc = bank("g_acc%d%d" % (j, u), banks[u])
+                for w in range(2):
+                    slot = slice((2 * u + w) * P, (2 * u + w + 1) * P)
+                    for lg in range(GROUPS):
+                        nc.tensor.matmul_mx(
+                            out=acc[:, w * AW : (w + 1) * AW],
+                            lhsT=t["b_codes%d%d" % (lg, g)][:, slot].bitcast(E4M3),
+                            lhsT_scale=t["b_sc%d%d" % (lg, g)][:, slot],
+                            rhs=t["a_codes%d" % a_steps.index((q, lg))][:].bitcast(E4M3),
+                            rhs_scale=t["a_sc%d" % a_steps.index((q, lg))][:],
+                            start=(lg == 0),
+                            stop=(lg == GROUPS - 1),
+                        )
+
+        def y_finish(j, u):
+            q, g = g_steps[j]
+            half, part = divmod(q, 2)
+            if u == 0:
+                rotating("y_t", "y_t%d" % j, [P, PACK, AW], F32, 3)
+            for w in range(2):
+                tc_ = 2 * u + w
+                nc.vector.scalar_tensor_tensor(
+                    out=t["y_t%d" % j][:, tc_, :],
+                    in0=t["g_acc%d%d" % (j, u)][:, w * AW : (w + 1) * AW],
+                    scalar=t["step"][:, g, tc_ : tc_ + 1],
+                    in1=t["rps%d%d%d" % (half, g, tc_)][:, part * AW : (part + 1) * AW],
+                    op0=MULT,
+                    op1=ADD,
+                )
+
+        def y_group(j, engine, cols):
+            if "y_grp%d" % j not in t:
+                rotating("y_grp", "y_grp%d" % j, [P, AW, PACK], BF16, 2)
+            copy_on(
+                engine,
+                t["y_grp%d" % j][:, cols, :].rearrange("p (c i) s -> p c s i", i=4),
+                t["y_t%d" % j][:, :, cols].rearrange("p s (c i) -> p c s i", i=4),
+            )
+
+        y_sc = kept("y_sc", [P, GROUPS, SIZE], U8)
+
+        def y_quantize(j):
+            q, g = g_steps[j]
+            codes = rotating("y_codes", "y_codes%d" % j, [P, AW], U32, 3)
+            quantize(codes[:], y_sc[:, g, q * AW : (q + 1) * AW], t["y_grp%d" % j][:].rearrange("p a s -> p (a s)"))
+
+        def y_store_codes(j):
+            q, g = g_steps[j]
+            codes = t["y_codes%d" % j]
+            nc.sync.dma_start(
+                out=out_1[g, :, q * AW : (q + 1) * AW, :].rearrange("p a s -> p (a s)").bitcast(I32),
+                in_=codes[:].bitcast(I32),
+            )
+
+        def y_transposes(j, banks):
+            for i in range(AW // P):
+                acc = bank("y_turned%d%d" % (j, i), banks[i])
+                for tc_ in range(PACK):
+                    nc.tensor.transpose(
+                        acc[:, tc_ * P : (tc_ + 1) * P], t["y_t%d" % j][:, tc_, i * P : (i + 1) * P], ident[:]
+                    )
+
+        def y_store(j):
+            q, g = g_steps[j]
+            for i in range(AW // P):
+                rows = rotating("y_rows", "y_rows%d%d" % (j, i), [P, P, PACK], F32, 6)
+                nc.scalar.copy(out=rows[:], in_=t["y_turned%d%d" % (j, i)][:].rearrange("a (s p) -> a p s", s=PACK))
+                a0 = q * AW + i * P
+                nc.sync.dma_start(
+                    out=out_0[a0 : a0 + P, g * KP : (g + 1) * KP], in_=rows[:].rearrange("a p s -> a (p s)")
+                )
+
+        S, V = nc.scalar, nc.vector
+        r_units = [(half, g, u) for half in range(2) for g in range(GROUPS) for u in range(2)]
+        a_steps = [(0, 0), (1, 0), (0, 1), (1, 1), (2, 0), (2, 1), (3, 0), (3, 1)]
+        g_steps = [(0, 0), (0, 1), (1, 0), (1, 1), (2, 0), (2, 1), (3, 0), (3, 1)]
+        both = [(V, slice(0, 3)), (S, slice(3, 4))]
+        group_d(0, 0, both)
+        quantize_input("d", 0, 0)
+        group_d(1, 0, both)
+        quantize_input("d", 1, 0)
+        group_d(0, 1, both)
+        group_d(1, 1, [(S, slice(0, 4))])
+        group_x(0, 0, S)
+        for k in range(4):
+            b_matmuls(k, k)
+        for k in range(12):
+            if k == 1:
+                quantize_input("d", 0, 1)
+                group_x(1, 0, S)
+            if k == 4:
+                quantize_input("d", 1, 1)
+                group_x(0, 1, S)
+            if k == 7:
+                quantize_input("x", 0, 0)
+                group_x(1, 1, S)
+            if k == 11:
+                quantize_input("x", 1, 0)
+            b_add(k)
+            if k + 4 < 14:
+                b_matmuls(k + 4, k % 4)
+            if k == 9:
+                for n in range(4):
+                    r_transposes(n, 4 + n)
+            if k % 4 == 1 and k > 1:
+                b_quantize(*divmod(k // 4 - 1, GROUPS))
+        ps = kept("ps", [P, GROUPS, PACK], F32)
+        nc.vector.tensor_tensor(out=ps[:], in0=t["penalty"][:], in1=t["step"][:], op=MULT)
+
+        a_matmuls(0, (2, 3))
+        b_add(12)
+        b_quantize(1, 0)
+        b_add(13)
+        a_matmuls(1, (0, 1))
+        a_add(0, 0)
+        quantize_input("x", 0, 1)
+        a_add(0, 1)
+        quantize_input("x", 1, 1)
+        r_scale(0)
+        r_scale(1)
+        a_matmuls(2, (2, 3))
+        a_transposes(0, 4)
+        a_add(1, 0)
+        a_add(1, 1)
+        a_copy(0)
+        r_scale(2)
+        b_matmuls(14, 0)
+        b_matmuls(15, 1)
+        a_add(2, 0)
+        a_add(2, 1)
+        a_transposes(1, 4)
+        a_transposes(2, 5)
+        a_copy(1)
+        a_quantize(0)
+        a_copy(2)
+        a_matmuls(3, (2, 3))
+        b_add(14)
+        a_quantize(1)
+        b_add(15)
+        a_quantize(2)
+        r_scale(3)
+        a_add(3, 0)
+        a_add(3, 1)
+
+        steps = len(g_steps)
+        for j in range(steps + 1):
+            s = j + 4
+            late = j >= 4 and j % 2 == 1
+            if 1 <= j < steps:
+                y_group(j - 1, S, slice(AW // 2, AW))
+            if j < steps:
+                g_matmuls(j, (0, 1) if late else (4, 5))
+            if s < steps:
+                a_matmuls(s, (0, 1))
+            if 1 <= j:
+                y_transposes(j - 1, (2, 7) if j >= 6 and j % 2 == 0 else (3, 6))
+            if s - 1 < steps:
+                a_transposes(s - 1, 2)
+            if s < len(r_units):
+                r_transposes(s, 7)
+            if j < steps:
+                y_finish(j, 0)
+            if j == 0:
+                b_quantize(1, 1)
+            if 1 <= j:
+                y_group(j - 1, V, slice(0, AW // 2 if j < steps else AW))
+            if 3 <= s - 2 < steps:
+                a_quantize(s - 2)
+            if j < steps:
+                y_finish(j, 1)
+            if s < steps:
+                a_add(s, 0)
+            if 1 <= j:
+                y_quantize(j - 1)
+            if s < steps:
+                a_add(s, 1)
+            if 1 <= j:
+                y_store(j - 1)
+                y_store_codes(j - 1)
+            if s - 1 < steps:
+                a_copy(s - 1)
+            if s < len(r_units):
+                r_scale(s)
+
+        for quad in range(4):
+            nc.sync.dma_start(
+                out=out_2[:, 4 * quad : 4 * quad + 4, :].rearrange("g r n -> r g n").bitcast(I32),
+                in_=y_sc[32 * quad : 32 * quad + 4, :, :].bitcast(I32),
+            )

@@ -54,7 +54,7 @@ def tile_qap_reassignment_gradient_k4_kernel(
                 engine.tensor_copy(out=out, in_=in_)
 
         def load_rows(name, src, kg, lg):
-            raw = kept("%s_raw%d%d" % (name, kg, lg), [P, PACK, KP], BF16)
+            raw = rotating("raw", "%s_raw%d%d" % (name, kg, lg), [P, PACK, KP], BF16, 8)
             rows = src[kg * KP : (kg + 1) * KP, lg * KP : (lg + 1) * KP]
             nc.sync.dma_start(out=raw[:], in_=rows.rearrange("(p s) l -> p s l", s=PACK))
 
@@ -71,38 +71,40 @@ def tile_qap_reassignment_gradient_k4_kernel(
         nc.vector.memset(z_sc[:].rearrange("p g n -> p (g n)").bitcast(I32), 0)
         nc.vector.memset(f_sc[:].rearrange("p g n -> p (g n)").bitcast(I32), 0)
 
-        def load_scales(plane, src):
+        def load_scales(queue, plane, src):
             for quad in range(4):
-                nc.sync.dma_start(
+                queue.dma_start(
                     out=plane[32 * quad : 32 * quad + 4, :, :].bitcast(I32),
                     in_=src[:, 4 * quad : 4 * quad + 4, :].rearrange("g r n -> r g n").bitcast(I32),
                 )
 
-        def load_z(g):
-            zc = kept("z_codes%d" % g, [P, GROUPS, KP], I32)
-            words = z_words[:, :, g * KP : (g + 1) * KP, :].rearrange("j p n t -> p j (n t)")
+        def load_z(n):
+            zc = kept("z_codes%d" % n, [P, GROUPS, 2 * P], I32)
+            words = z_words[:, :, 2 * n * P : 2 * (n + 1) * P, :].rearrange("j p n t -> p j (n t)")
             nc.sync.dma_start(out=zc[:], in_=words.bitcast(I32))
 
         ident = kept("ident", [P, P], F32)
         make_identity(nc, ident[:])
+        load_scales(nc.gpsimd, f_sc, f_scales)
 
         load_rows("d", d, 0, 0)
         load_rows("d", d, 1, 0)
-        load_scales(z_sc, z_scales)
-        load_z(0)
+        load_scales(nc.sync, z_sc, z_scales)
         load_rows("d", d, 0, 1)
-        load_vector("h", h)
+        load_z(0)
         load_rows("d", d, 1, 1)
+        load_vector("h", h)
         load_z(1)
         load_rows("x", x, 0, 0)
+        load_z(2)
+        load_z(3)
         load_rows("x", x, 1, 0)
-        load_tiles("r", r, 0)
-        load_tiles("r", r, 1)
         load_rows("x", x, 0, 1)
-        load_scales(f_sc, f_scales)
+        load_tiles("r", r, 0)
+        load_rows("x", x, 1, 1)
+        load_tiles("r", r, 1)
         f_codes = kept("f_codes", [P, GROUPS, 2 * SIZE], U8)
         nc.sync.dma_start(out=f_codes[:].bitcast(I32), in_=f_words.rearrange("g p n -> p g n").bitcast(I32))
-        load_rows("x", x, 1, 1)
         load_vector("step", step)
         load_vector("penalty", penalty)
         load_tiles("e", e, 0)
@@ -148,7 +150,7 @@ def tile_qap_reassignment_gradient_k4_kernel(
                         out=acc[:, slot],
                         lhsT=t["d_codes%d%d" % (jg, lg)][:, slot].bitcast(E4M3),
                         lhsT_scale=t["d_sc%d%d" % (jg, lg)][:, slot],
-                        rhs=t["z_codes%d" % (n // 4)][:, jg, n % 4 * P : (n % 4 + 1) * P].bitcast(E4M3),
+                        rhs=t["z_codes%d" % (n // 2)][:, jg, n % 2 * P : (n % 2 + 1) * P].bitcast(E4M3),
                         rhs_scale=z_sc[:, jg, cols],
                         start=(jg == 0),
                         stop=(jg == GROUPS - 1),
@@ -176,8 +178,17 @@ def tile_qap_reassignment_gradient_k4_kernel(
             half, g, u = r_units[n]
             acc = bank("r_acc%d%d%d" % (half, g, u), index)
             for i in range(4):
-                words = t["r_raw%d" % (2 * half + i // 2)][:, i % 2, :].bitcast(F32)
-                nc.tensor.transpose(acc[:, i * P : (i + 1) * P], words[:, 256 * g + u : 256 * (g + 1) : 2], ident[:])
+                q = 2 * half + i // 2
+                if "r_sorted%d" % q in t:
+                    words = t["r_sorted%d" % q][:, i % 2, g, u, :]
+                else:
+                    words = t["r_raw%d" % q][:, i % 2, :].bitcast(F32)[:, 256 * g + u : 256 * (g + 1) : 2]
+                nc.tensor.transpose(acc[:, i * P : (i + 1) * P], words, ident[:])
+
+        def r_sort(q):
+            dst = rotating("raw", "r_sorted%d" % q, [P, AW // P, GROUPS, 2, P], F32, 8)
+            words = t["r_raw%d" % q][:].bitcast(F32).rearrange("a i (g p u) -> a i g u p", g=GROUPS, u=2)
+            nc.scalar.copy(out=dst[:], in_=words)
 
         def r_scale(n):
             half, g, u = r_units[n]
@@ -222,7 +233,7 @@ def tile_qap_reassignment_gradient_k4_kernel(
                     nc.tensor.transpose(acc[:, col : col + P], words[:, u * P : (u + 1) * P], ident[:])
 
         def a_copy(s):
-            grp = rotating("a_grp", "a_grp%d" % s, [P, AW * PACK], BF16, 2)
+            grp = rotating("a_grp", "a_grp%d" % s, [P, AW * PACK], BF16, 3)
             nc.scalar.copy(
                 out=grp[:].bitcast(F32).rearrange("p (a u) -> p a u", u=2),
                 in_=t["a_turned%d" % s][:].rearrange("p (u a) -> p a u", u=2),
@@ -234,41 +245,47 @@ def tile_qap_reassignment_gradient_k4_kernel(
             quantize(codes[:], scales[:], t["a_grp%d" % s][:])
 
         def g_matmuls(j, banks):
-            q, g = g_steps[j]
-            for u in range(2):
-                acc = bank("g_acc%d%d" % (j, u), banks[u])
-                for w in range(2):
-                    slot = slice((2 * u + w) * P, (2 * u + w + 1) * P)
-                    for lg in range(GROUPS):
-                        nc.tensor.matmul_mx(
-                            out=acc[:, w * AW : (w + 1) * AW],
-                            lhsT=t["b_codes%d%d" % (lg, g)][:, slot].bitcast(E4M3),
-                            lhsT_scale=t["b_sc%d%d" % (lg, g)][:, slot],
-                            rhs=t["a_codes%d" % a_steps.index((q, lg))][:].bitcast(E4M3),
-                            rhs_scale=t["a_sc%d" % a_steps.index((q, lg))][:],
-                            start=(lg == 0),
-                            stop=(lg == GROUPS - 1),
-                        )
+            a0, width, g = g_steps[j]
+            q, within = divmod(a0, AW)
+            cols = slice(within, within + width)
+            for tc_ in range(PACK):
+                n, place = divmod(tc_ * width, KP)
+                if place == 0:
+                    acc = bank("g_acc%d%d" % (j, n), banks[n])
+                slot = slice(tc_ * P, (tc_ + 1) * P)
+                for lg in range(GROUPS):
+                    s = a_steps.index((q, lg))
+                    nc.tensor.matmul_mx(
+                        out=acc[:, place : place + width],
+                        lhsT=t["b_codes%d%d" % (lg, g)][:, slot].bitcast(E4M3),
+                        lhsT_scale=t["b_sc%d%d" % (lg, g)][:, slot],
+                        rhs=t["a_codes%d" % s][:, cols].bitcast(E4M3),
+                        rhs_scale=t["a_sc%d" % s][:, cols],
+                        start=(lg == 0),
+                        stop=(lg == GROUPS - 1),
+                    )
 
         def y_finish(j, u):
-            q, g = g_steps[j]
-            half, part = divmod(q, 2)
+            a0, width, g = g_steps[j]
+            half, within = divmod(a0, KP)
             if u == 0:
-                rotating("y_t", "y_t%d" % j, [P, PACK, AW], F32, 3)
-            for w in range(2):
-                tc_ = 2 * u + w
+                rotating("y_t", "y_t%d" % j, [P, PACK, width], F32, 3)
+            for tc_ in (2 * u, 2 * u + 1):
+                n, place = divmod(tc_ * width, KP)
                 nc.vector.scalar_tensor_tensor(
                     out=t["y_t%d" % j][:, tc_, :],
-                    in0=t["g_acc%d%d" % (j, u)][:, w * AW : (w + 1) * AW],
+                    in0=t["g_acc%d%d" % (j, n)][:, place : place + width],
                     scalar=t["step"][:, g, tc_ : tc_ + 1],
-                    in1=t["rps%d%d%d" % (half, g, tc_)][:, part * AW : (part + 1) * AW],
+                    in1=t["rps%d%d%d" % (half, g, tc_)][:, within : within + width],
                     op0=MULT,
                     op1=ADD,
                 )
 
-        def y_group(j, engine, cols):
+        def y_group(j, engine, first, last):
+            width = g_steps[j][1]
+            cols = slice(first * width // 8, last * width // 8)
             if "y_grp%d" % j not in t:
-                rotating("y_grp", "y_grp%d" % j, [P, AW, PACK], BF16, 2)
+                rotating("y_grp", "y_grp%d" % j, [P, width, PACK], BF16, 3)
             copy_on(
                 engine,
                 t["y_grp%d" % j][:, cols, :].rearrange("p (c i) s -> p c s i", i=4),
@@ -276,22 +293,23 @@ def tile_qap_reassignment_gradient_k4_kernel(
             )
 
         y_sc = kept("y_sc", [P, GROUPS, SIZE], U8)
+        y_codes = [kept("y_codes%d" % g, [P, SIZE], U32) for g in range(GROUPS)]
 
         def y_quantize(j):
-            q, g = g_steps[j]
-            codes = rotating("y_codes", "y_codes%d" % j, [P, AW], U32, 3)
-            quantize(codes[:], y_sc[:, g, q * AW : (q + 1) * AW], t["y_grp%d" % j][:].rearrange("p a s -> p (a s)"))
+            a0, width, g = g_steps[j]
+            cols = slice(a0, a0 + width)
+            quantize(y_codes[g][:, cols], y_sc[:, g, cols], t["y_grp%d" % j][:].rearrange("p a s -> p (a s)"))
 
         def y_store_codes(j):
-            q, g = g_steps[j]
-            codes = t["y_codes%d" % j]
+            a0, g = g_steps[j][0], g_steps[j][2]
+            cols = slice(a0, a0 + AW)
             nc.sync.dma_start(
-                out=out_1[g, :, q * AW : (q + 1) * AW, :].rearrange("p a s -> p (a s)").bitcast(I32),
-                in_=codes[:].bitcast(I32),
+                out=out_1[g, :, cols, :].rearrange("p a s -> p (a s)").bitcast(I32),
+                in_=y_codes[g][:, cols].bitcast(I32),
             )
 
         def y_transposes(j, banks):
-            for i in range(AW // P):
+            for i in range(g_steps[j][1] // P):
                 acc = bank("y_turned%d%d" % (j, i), banks[i])
                 for tc_ in range(PACK):
                     nc.tensor.transpose(
@@ -299,26 +317,27 @@ def tile_qap_reassignment_gradient_k4_kernel(
                     )
 
         def y_store(j):
-            q, g = g_steps[j]
-            for i in range(AW // P):
+            a0, width, g = g_steps[j]
+            for i in range(width // P):
                 rows = rotating("y_rows", "y_rows%d%d" % (j, i), [P, P, PACK], F32, 6)
                 nc.scalar.copy(out=rows[:], in_=t["y_turned%d%d" % (j, i)][:].rearrange("a (s p) -> a p s", s=PACK))
-                a0 = q * AW + i * P
                 nc.sync.dma_start(
-                    out=out_0[a0 : a0 + P, g * KP : (g + 1) * KP], in_=rows[:].rearrange("a p s -> a (p s)")
+                    out=out_0[a0 + i * P : a0 + (i + 1) * P, g * KP : (g + 1) * KP],
+                    in_=rows[:].rearrange("a p s -> a (p s)"),
                 )
 
         S, V = nc.scalar, nc.vector
         r_units = [(half, g, u) for half in range(2) for g in range(GROUPS) for u in range(2)]
         a_steps = [(0, 0), (1, 0), (0, 1), (1, 1), (2, 0), (2, 1), (3, 0), (3, 1)]
-        g_steps = [(0, 0), (0, 1), (1, 0), (1, 1), (2, 0), (2, 1), (3, 0), (3, 1)]
+        g_steps = [(q * AW, AW, g) for q in range(SIZE // AW) for g in range(GROUPS)][:-1]
+        g_steps.extend([(SIZE - 2 * P, P, 1), (SIZE - P, P, 1)])
         both = [(V, slice(0, 3)), (S, slice(3, 4))]
         group_d(0, 0, both)
         quantize_input("d", 0, 0)
-        group_d(1, 0, both)
+        group_d(1, 0, [(S, slice(2, 4)), (V, slice(0, 2))])
         quantize_input("d", 1, 0)
-        group_d(0, 1, both)
-        group_d(1, 1, [(S, slice(0, 4))])
+        group_d(0, 1, [(S, slice(0, 4))])
+        group_d(1, 1, both)
         group_x(0, 0, S)
         for k in range(4):
             b_matmuls(k, k)
@@ -326,13 +345,13 @@ def tile_qap_reassignment_gradient_k4_kernel(
             if k == 1:
                 quantize_input("d", 0, 1)
                 group_x(1, 0, S)
-            if k == 4:
+            if k == 3:
                 quantize_input("d", 1, 1)
                 group_x(0, 1, S)
-            if k == 7:
+            if k == 6:
                 quantize_input("x", 0, 0)
                 group_x(1, 1, S)
-            if k == 11:
+            if k == 10:
                 quantize_input("x", 1, 0)
             b_add(k)
             if k + 4 < 14:
@@ -347,78 +366,81 @@ def tile_qap_reassignment_gradient_k4_kernel(
 
         a_matmuls(0, (2, 3))
         b_add(12)
-        b_quantize(1, 0)
-        b_add(13)
-        a_matmuls(1, (0, 1))
-        a_add(0, 0)
         quantize_input("x", 0, 1)
-        a_add(0, 1)
-        quantize_input("x", 1, 1)
+        b_add(13)
+        b_quantize(1, 0)
+        a_matmuls(1, (0, 1))
         r_scale(0)
         r_scale(1)
-        a_matmuls(2, (2, 3))
+        r_sort(2)
+        a_add(0, 0)
+        a_add(0, 1)
+        quantize_input("x", 1, 1)
         a_transposes(0, 4)
+        a_matmuls(2, (2, 3))
         a_add(1, 0)
         a_add(1, 1)
         a_copy(0)
         r_scale(2)
         b_matmuls(14, 0)
-        b_matmuls(15, 1)
         a_add(2, 0)
         a_add(2, 1)
         a_transposes(1, 4)
         a_transposes(2, 5)
-        a_copy(1)
-        a_quantize(0)
         a_copy(2)
+        a_copy(1)
+        b_matmuls(15, 1)
         a_matmuls(3, (2, 3))
+        a_quantize(0)
         b_add(14)
-        a_quantize(1)
-        b_add(15)
         a_quantize(2)
+        b_add(15)
         r_scale(3)
+        r_sort(3)
         a_add(3, 0)
+        a_quantize(1)
         a_add(3, 1)
 
         steps = len(g_steps)
-        for j in range(steps + 1):
+        for j in range(steps):
             s = j + 4
-            late = j >= 4 and j % 2 == 1
-            if 1 <= j < steps:
-                y_group(j - 1, S, slice(AW // 2, AW))
-            if j < steps:
-                g_matmuls(j, (0, 1) if late else (4, 5))
-            if s < steps:
+            if 1 <= j < steps - 1:
+                y_group(j - 1, S, 5, 8)
+            g_matmuls(j, (0, 1) if j >= 4 and j % 2 == 1 else (4, 5))
+            if s < len(a_steps):
                 a_matmuls(s, (0, 1))
-            if 1 <= j:
-                y_transposes(j - 1, (2, 7) if j >= 6 and j % 2 == 0 else (3, 6))
-            if s - 1 < steps:
+            if s - 1 < len(a_steps):
                 a_transposes(s - 1, 2)
+                a_copy(s - 1)
+            if 1 <= j:
+                y_transposes(j - 1, (2, 7) if j >= 5 and j % 2 == 1 else (3, 6))
+                y_store(j - 1)
             if s < len(r_units):
                 r_transposes(s, 7)
-            if j < steps:
-                y_finish(j, 0)
+                r_scale(s)
+            y_finish(j, 0)
             if j == 0:
                 b_quantize(1, 1)
-            if 1 <= j:
-                y_group(j - 1, V, slice(0, AW // 2 if j < steps else AW))
-            if 3 <= s - 2 < steps:
+            if 3 <= s - 2 < len(a_steps):
                 a_quantize(s - 2)
-            if j < steps:
-                y_finish(j, 1)
-            if s < steps:
+            if 2 <= j < steps - 1:
+                y_quantize(j - 2)
+                y_store_codes(j - 2)
+            y_finish(j, 1)
+            if 1 <= j < steps - 1:
+                y_group(j - 1, V, 0, 5)
+            if s < len(a_steps):
                 a_add(s, 0)
-            if 1 <= j:
-                y_quantize(j - 1)
-            if s < steps:
                 a_add(s, 1)
-            if 1 <= j:
-                y_store(j - 1)
-                y_store_codes(j - 1)
-            if s - 1 < steps:
-                a_copy(s - 1)
-            if s < len(r_units):
-                r_scale(s)
+        y_group(steps - 2, S, 0, 8)
+        y_quantize(steps - 3)
+        y_store_codes(steps - 3)
+        y_group(steps - 1, V, 0, 8)
+        y_transposes(steps - 1, (2, 7))
+        y_quantize(steps - 2)
+        y_quantize(steps - 1)
+        y_store(steps - 1)
+        y_store_codes(steps - 2)
 
         for quad in range(4):
             nc.sync.dma_start(

@@ -62,6 +62,10 @@ def tile_qap_reassignment_gradient_k4_kernel(
             raw = kept("%s_raw%d" % (name, q), [P, AW // P, SIZE], BF16)
             nc.sync.dma_start(out=raw[:], in_=src[q * AW : (q + 1) * AW, :].rearrange("(i p) n -> p i n", p=P))
 
+        def load_r(half):
+            raw = kept("r_raw%d" % half, [P, 4, SIZE], BF16)
+            nc.sync.dma_start(out=raw[:], in_=r[half * KP : (half + 1) * KP, :].rearrange("(p i) c -> p i c", i=4))
+
         def load_vector(name, src):
             v = kept(name, [P, GROUPS, PACK], BF16)
             nc.sync.dma_start(out=v[:], in_=src.rearrange("(g p t) -> p g t", p=P, t=PACK))
@@ -85,32 +89,30 @@ def tile_qap_reassignment_gradient_k4_kernel(
 
         ident = kept("ident", [P, P], F32)
         make_identity(nc, ident[:])
-        load_scales(nc.gpsimd, f_sc, f_scales)
 
         load_rows("d", d, 0, 0)
         load_rows("d", d, 1, 0)
         load_scales(nc.sync, z_sc, z_scales)
         load_rows("d", d, 0, 1)
         load_z(0)
-        load_rows("d", d, 1, 1)
         load_vector("h", h)
+        load_rows("d", d, 1, 1)
         load_z(1)
         load_rows("x", x, 0, 0)
         load_z(2)
         load_z(3)
+        load_vector("step", step)
         load_rows("x", x, 1, 0)
+        load_vector("penalty", penalty)
         load_rows("x", x, 0, 1)
-        load_tiles("r", r, 0)
+        load_r(0)
         load_rows("x", x, 1, 1)
-        load_tiles("r", r, 1)
+        load_scales(nc.sync, f_sc, f_scales)
         f_codes = kept("f_codes", [P, GROUPS, 2 * SIZE], U8)
         nc.sync.dma_start(out=f_codes[:].bitcast(I32), in_=f_words.rearrange("g p n -> p g n").bitcast(I32))
-        load_vector("step", step)
-        load_vector("penalty", penalty)
         load_tiles("e", e, 0)
         load_tiles("e", e, 1)
-        load_tiles("r", r, 2)
-        load_tiles("r", r, 3)
+        load_r(1)
         load_tiles("e", e, 2)
         load_tiles("e", e, 3)
 
@@ -118,14 +120,20 @@ def tile_qap_reassignment_gradient_k4_kernel(
             grp = rotating("grp", "d_grp%d%d" % (jg, lg), [P, PACK, P, PACK], BF16, 4)
             raw = t["d_raw%d%d" % (jg, lg)][:].rearrange("p s (m t) -> p m s t", t=PACK)
             for engine, slots in shares:
-                copy_on(engine, grp[:, slots].rearrange("p t m s -> p m s t"), raw[:, :, :, slots])
+                out, in_ = grp[:, slots].rearrange("p t m s -> p m s t"), raw[:, :, :, slots]
+                if (jg, lg) == (0, 0) and engine is nc.scalar:
+                    nc.scalar.activation(out=out, in_=in_, func=COPY)
+                else:
+                    copy_on(engine, out, in_)
 
-        def group_x(bg, lg, engine):
-            grp = rotating("grp", "x_grp%d%d" % (bg, lg), [P, KP, PACK], BF16, 4)
+        def group_x(bg, lg, engine, cols=slice(0, KP)):
+            name = "x_grp%d%d" % (bg, lg)
+            if name not in t:
+                rotating("grp", name, [P, KP, PACK], BF16, 4)
             copy_on(
                 engine,
-                grp[:].rearrange("p (c i) s -> p c s i", i=4),
-                t["x_raw%d%d" % (bg, lg)][:].rearrange("p s (c i) -> p c s i", i=4),
+                t[name][:, cols, :].rearrange("p (c i) s -> p c s i", i=4),
+                t["x_raw%d%d" % (bg, lg)][:, :, cols].rearrange("p s (c i) -> p c s i", i=4),
             )
 
         def quantize(codes, scales, values):
@@ -176,27 +184,31 @@ def tile_qap_reassignment_gradient_k4_kernel(
 
         def r_transposes(n, index):
             half, g, u = r_units[n]
-            acc = bank("r_acc%d%d%d" % (half, g, u), index)
+            acc = bank("r_acc%d" % n, index)
             for i in range(4):
-                q = 2 * half + i // 2
-                if "r_sorted%d" % q in t:
-                    words = t["r_sorted%d" % q][:, i % 2, g, u, :]
+                if half == 1:
+                    words = t["r_sorted%d" % g][:, i, u, :]
                 else:
-                    words = t["r_raw%d" % q][:, i % 2, :].bitcast(F32)[:, 256 * g + u : 256 * (g + 1) : 2]
+                    words = t["r_raw0"][:, i, :].bitcast(F32)[:, 256 * g + u : 256 * (g + 1) : 2]
                 nc.tensor.transpose(acc[:, i * P : (i + 1) * P], words, ident[:])
 
-        def r_sort(q):
-            dst = rotating("raw", "r_sorted%d" % q, [P, AW // P, GROUPS, 2, P], F32, 8)
-            words = t["r_raw%d" % q][:].bitcast(F32).rearrange("a i (g p u) -> a i g u p", g=GROUPS, u=2)
-            nc.scalar.copy(out=dst[:], in_=words)
+        def r_sort(g):
+            dst = rotating("raw", "r_sorted%d" % g, [P, 4, 2, P], F32, 8)
+            words = t["r_raw1"][:, :, g * KP : (g + 1) * KP].bitcast(F32).rearrange("a i (p u) -> a i p u", u=2)
+            nc.scalar.copy(out=dst[:].rearrange("a i u p -> a i p u"), in_=words)
 
         def r_scale(n):
             half, g, u = r_units[n]
-            pairs = t["r_acc%d%d%d" % (half, g, u)][:].bitcast(BF16).rearrange("p (a w) -> p a w", w=2)
+            pairs = t["r_acc%d" % n][:].bitcast(BF16).rearrange("p (i m w) -> p m i w", i=4, w=2)
             for w in range(2):
                 tc_ = 2 * u + w
                 dst = kept("rps%d%d%d" % (half, g, tc_), [P, KP], F32)
-                nc.scalar.activation(out=dst[:], in_=pairs[:, :, w], func=COPY, scale=t["ps"][:, g, tc_ : tc_ + 1])
+                nc.scalar.activation(
+                    out=dst[:].rearrange("p (m i) -> p m i", i=4),
+                    in_=pairs[:, :, :, w],
+                    func=COPY,
+                    scale=t["ps"][:, g, tc_ : tc_ + 1],
+                )
 
         def a_matmuls(s, banks):
             q, lg = a_steps[s]
@@ -268,12 +280,13 @@ def tile_qap_reassignment_gradient_k4_kernel(
         def y_finish(j, u):
             a0, width, g = g_steps[j]
             half, within = divmod(a0, KP)
-            if u == 0:
-                rotating("y_t", "y_t%d" % j, [P, PACK, width], F32, 3)
+            if u == 0 and a0 % AW == 0:
+                rotating("y_t", "y_t%d%d" % (a0 // AW, g), [P, PACK, AW], F32, 3)
+            cols = slice(a0 % AW, a0 % AW + width)
             for tc_ in (2 * u, 2 * u + 1):
                 n, place = divmod(tc_ * width, KP)
                 nc.vector.scalar_tensor_tensor(
-                    out=t["y_t%d" % j][:, tc_, :],
+                    out=t["y_t%d%d" % (a0 // AW, g)][:, tc_, cols],
                     in0=t["g_acc%d%d" % (j, n)][:, place : place + width],
                     scalar=t["step"][:, g, tc_ : tc_ + 1],
                     in1=t["rps%d%d%d" % (half, g, tc_)][:, within : within + width],
@@ -282,22 +295,22 @@ def tile_qap_reassignment_gradient_k4_kernel(
                 )
 
         def y_group(j, engine, first, last):
-            width = g_steps[j][1]
-            cols = slice(first * width // 8, last * width // 8)
+            q, g = divmod(j, GROUPS)
+            cols = slice(first * AW // 8, last * AW // 8)
             if "y_grp%d" % j not in t:
-                rotating("y_grp", "y_grp%d" % j, [P, width, PACK], BF16, 3)
+                rotating("y_grp", "y_grp%d" % j, [P, AW, PACK], BF16, 3)
             copy_on(
                 engine,
                 t["y_grp%d" % j][:, cols, :].rearrange("p (c i) s -> p c s i", i=4),
-                t["y_t%d" % j][:, :, cols].rearrange("p s (c i) -> p c s i", i=4),
+                t["y_t%d%d" % (q, g)][:, :, cols].rearrange("p s (c i) -> p c s i", i=4),
             )
 
         y_sc = kept("y_sc", [P, GROUPS, SIZE], U8)
         y_codes = [kept("y_codes%d" % g, [P, SIZE], U32) for g in range(GROUPS)]
 
         def y_quantize(j):
-            a0, width, g = g_steps[j]
-            cols = slice(a0, a0 + width)
+            q, g = divmod(j, GROUPS)
+            cols = slice(q * AW, (q + 1) * AW)
             quantize(y_codes[g][:, cols], y_sc[:, g, cols], t["y_grp%d" % j][:].rearrange("p a s -> p (a s)"))
 
         def y_store_codes(j):
@@ -309,11 +322,13 @@ def tile_qap_reassignment_gradient_k4_kernel(
             )
 
         def y_transposes(j, banks):
-            for i in range(g_steps[j][1] // P):
+            a0, width, g = g_steps[j]
+            for i in range(width // P):
                 acc = bank("y_turned%d%d" % (j, i), banks[i])
+                cols = slice(a0 % AW + i * P, a0 % AW + (i + 1) * P)
                 for tc_ in range(PACK):
                     nc.tensor.transpose(
-                        acc[:, tc_ * P : (tc_ + 1) * P], t["y_t%d" % j][:, tc_, i * P : (i + 1) * P], ident[:]
+                        acc[:, tc_ * P : (tc_ + 1) * P], t["y_t%d%d" % (a0 // AW, g)][:, tc_, cols], ident[:]
                     )
 
         def y_store(j):
@@ -336,8 +351,8 @@ def tile_qap_reassignment_gradient_k4_kernel(
         quantize_input("d", 0, 0)
         group_d(1, 0, [(S, slice(2, 4)), (V, slice(0, 2))])
         quantize_input("d", 1, 0)
-        group_d(0, 1, [(S, slice(0, 4))])
-        group_d(1, 1, both)
+        group_d(0, 1, both)
+        group_d(1, 1, [(S, slice(0, 4))])
         group_x(0, 0, S)
         for k in range(4):
             b_matmuls(k, k)
@@ -345,20 +360,20 @@ def tile_qap_reassignment_gradient_k4_kernel(
             if k == 1:
                 quantize_input("d", 0, 1)
                 group_x(1, 0, S)
-            if k == 3:
+            if k == 4:
                 quantize_input("d", 1, 1)
                 group_x(0, 1, S)
-            if k == 6:
+            if k == 8:
                 quantize_input("x", 0, 0)
                 group_x(1, 1, S)
-            if k == 10:
+            if k == 11:
                 quantize_input("x", 1, 0)
             b_add(k)
             if k + 4 < 14:
                 b_matmuls(k + 4, k % 4)
             if k == 9:
-                for n in range(4):
-                    r_transposes(n, 4 + n)
+                r_transposes(0, 4)
+                r_transposes(1, 5)
             if k % 4 == 1 and k > 1:
                 b_quantize(*divmod(k // 4 - 1, GROUPS))
         ps = kept("ps", [P, GROUPS, PACK], F32)
@@ -372,10 +387,10 @@ def tile_qap_reassignment_gradient_k4_kernel(
         a_matmuls(1, (0, 1))
         r_scale(0)
         r_scale(1)
-        r_sort(2)
         a_add(0, 0)
         a_add(0, 1)
         quantize_input("x", 1, 1)
+        r_transposes(2, 6)
         a_transposes(0, 4)
         a_matmuls(2, (2, 3))
         a_add(1, 0)
@@ -385,6 +400,7 @@ def tile_qap_reassignment_gradient_k4_kernel(
         b_matmuls(14, 0)
         a_add(2, 0)
         a_add(2, 1)
+        r_transposes(3, 7)
         a_transposes(1, 4)
         a_transposes(2, 5)
         a_copy(2)
@@ -396,7 +412,8 @@ def tile_qap_reassignment_gradient_k4_kernel(
         a_quantize(2)
         b_add(15)
         r_scale(3)
-        r_sort(3)
+        r_sort(0)
+        r_sort(1)
         a_add(3, 0)
         a_quantize(1)
         a_add(3, 1)
@@ -432,13 +449,11 @@ def tile_qap_reassignment_gradient_k4_kernel(
             if s < len(a_steps):
                 a_add(s, 0)
                 a_add(s, 1)
-        y_group(steps - 2, S, 0, 8)
         y_quantize(steps - 3)
         y_store_codes(steps - 3)
-        y_group(steps - 1, V, 0, 8)
+        y_group(steps - 2, V, 0, 8)
         y_transposes(steps - 1, (2, 7))
         y_quantize(steps - 2)
-        y_quantize(steps - 1)
         y_store(steps - 1)
         y_store_codes(steps - 2)
 

from contextlib import ExitStack

import concourse.mybir as mybir
from concourse.masks import make_identity

F32 = mybir.dt.float32
BF16 = mybir.dt.bfloat16
U32 = mybir.dt.uint32
I32 = mybir.dt.int32
U8 = mybir.dt.uint8
E4M3 = mybir.dt.float8_e4m3fn_x4
E2M1 = mybir.dt.float4_e2m1fn_x4
ADD = mybir.AluOpType.add
MULT = mybir.AluOpType.mult
COPY = mybir.ActivationFunctionType.Copy

SIZE = 1024
P = 128
PACK = 4
KP = P * PACK
GROUPS = SIZE // KP
AW = 256
FLOPS = 3 * 2 * SIZE * SIZE * SIZE


def tile_qap_reassignment_gradient_k4_kernel(
    tc, f_words, f_scales, x, e, z_words, z_scales, d, h, r, penalty, step, out_0, out_1, out_2
):
    nc = tc.nc
    with ExitStack() as ctx:
        keep = ctx.enter_context(tc.tile_pool(name="keep", bufs=1))
        work = ctx.enter_context(tc.tile_pool(name="work", bufs=1))
        psum = ctx.enter_context(tc.psum_pool(name="psum", bufs=1))
        ctx.enter_context(tc.manual_schedule())

        t = {}

        def kept(name, shape, dtype):
            t[name] = keep.tile(shape, dtype, name=name, align_bytes=64)
            return t[name]

        def rotating(tag, name, shape, dtype, bufs):
            t[name] = work.tile(shape, dtype, name=name, tag=tag, bufs=bufs, align_bytes=64)
            return t[name]

        def bank(name, index):
            t[name] = psum.tile([P, KP], F32, name=name, tag="bank%d" % index)
            return t[name]

        def copy_on(engine, out, in_):
            if engine is nc.scalar:
                nc.scalar.copy(out=out, in_=in_)
            else:
                engine.tensor_copy(out=out, in_=in_)

        def load_rows(name, src, kg, lg):
            raw = rotating("raw", "%s_raw%d%d" % (name, kg, lg), [P, PACK, KP], BF16, 8)
            rows = src[kg * KP : (kg + 1) * KP, lg * KP : (lg + 1) * KP]
            nc.sync.dma_start(out=raw[:], in_=rows.rearrange("(p s) l -> p s l", s=PACK))

        def load_tiles(name, src, q):
            raw = kept("%s_raw%d" % (name, q), [P, AW // P, SIZE], BF16)
            nc.sync.dma_start(out=raw[:], in_=src[q * AW : (q + 1) * AW, :].rearrange("(i p) n -> p i n", p=P))

        def load_r(half):
            raw = kept("r_raw%d" % half, [P, 4, SIZE], BF16)
            nc.sync.dma_start(out=raw[:], in_=r[half * KP : (half + 1) * KP, :].rearrange("(p i) c -> p i c", i=4))

        def load_vector(name, src):
            v = kept(name, [P, GROUPS, PACK], BF16)
            nc.sync.dma_start(out=v[:], in_=src.rearrange("(g p t) -> p g t", p=P, t=PACK))

        z_sc = kept("z_sc", [P, GROUPS, SIZE], U8)
        f_sc = kept("f_sc", [P, GROUPS, SIZE], U8)
        nc.vector.memset(z_sc[:].rearrange("p g n -> p (g n)").bitcast(I32), 0)
        nc.vector.memset(f_sc[:].rearrange("p g n -> p (g n)").bitcast(I32), 0)

        def load_scales(queue, plane, src):
            for quad in range(4):
                queue.dma_start(
                    out=plane[32 * quad : 32 * quad + 4, :, :].bitcast(I32),
                    in_=src[:, 4 * quad : 4 * quad + 4, :].rearrange("g r n -> r g n").bitcast(I32),
                )

        def load_z(n):
            zc = kept("z_codes%d" % n, [P, GROUPS, 2 * P], I32)
            words = z_words[:, :, 2 * n * P : 2 * (n + 1) * P, :].rearrange("j p n t -> p j (n t)")
            nc.sync.dma_start(out=zc[:], in_=words.bitcast(I32))

        ident = kept("ident", [P, P], F32)
        make_identity(nc, ident[:])

        load_rows("d", d, 0, 0)
        load_rows("d", d, 1, 0)
        load_scales(nc.sync, z_sc, z_scales)
        load_rows("d", d, 0, 1)
        load_z(0)
        load_vector("h", h)
        load_rows("d", d, 1, 1)
        load_z(1)
        load_rows("x", x, 0, 0)
        load_z(2)
        load_z(3)
        load_vector("step", step)
        load_rows("x", x, 1, 0)
        load_vector("penalty", penalty)
        load_rows("x", x, 0, 1)
        load_r(0)
        load_rows("x", x, 1, 1)
        load_scales(nc.sync, f_sc, f_scales)
        f_codes = kept("f_codes", [P, GROUPS, 2 * SIZE], U8)
        nc.sync.dma_start(out=f_codes[:].bitcast(I32), in_=f_words.rearrange("g p n -> p g n").bitcast(I32))
        load_tiles("e", e, 0)
        load_tiles("e", e, 1)
        load_r(1)
        load_tiles("e", e, 2)
        load_tiles("e", e, 3)

        def group_d(jg, lg, shares):
            grp = rotating("grp", "d_grp%d%d" % (jg, lg), [P, PACK, P, PACK], BF16, 4)
            raw = t["d_raw%d%d" % (jg, lg)][:].rearrange("p s (m t) -> p m s t", t=PACK)
            for engine, slots in shares:
                out, in_ = grp[:, slots].rearrange("p t m s -> p m s t"), raw[:, :, :, slots]
                if (jg, lg) == (0, 0) and engine is nc.scalar:
                    nc.scalar.activation(out=out, in_=in_, func=COPY)
                else:
                    copy_on(engine, out, in_)

        def group_x(bg, lg, engine, cols=slice(0, KP)):
            name = "x_grp%d%d" % (bg, lg)
            if name not in t:
                rotating("grp", name, [P, KP, PACK], BF16, 4)
            copy_on(
                engine,
                t[name][:, cols, :].rearrange("p (c i) s -> p c s i", i=4),
                t["x_raw%d%d" % (bg, lg)][:, :, cols].rearrange("p s (c i) -> p c s i", i=4),
            )

        def quantize(codes, scales, values):
            nc.vector.quantize_mx(out=codes.bitcast(E4M3), scales=scales, in_=values)

        def quantize_input(name, kg, lg):
            key = "%s_%s" + "%d%d" % (kg, lg)
            codes = kept(key % (name, "codes"), [P, KP], U32)
            scales = kept(key % (name, "sc"), [P, KP], U8)
            grp = t[key % (name, "grp")]
            flat = grp[:].rearrange("p t m s -> p (t m s)") if name == "d" else grp[:].rearrange("p c s -> p (c s)")
            quantize(codes[:], scales[:], flat)

        def b_matmuls(k, index):
            lg, n = divmod(k, 8)
            acc = bank("b_acc%d" % k, index)
            cols = slice(n * P, (n + 1) * P)
            for tl in range(PACK):
                slot = slice(tl * P, (tl + 1) * P)
                for jg in range(GROUPS):
                    nc.tensor.matmul_mx(
                        out=acc[:, slot],
                        lhsT=t["d_codes%d%d" % (jg, lg)][:, slot].bitcast(E4M3),
                        lhsT_scale=t["d_sc%d%d" % (jg, lg)][:, slot],
                        rhs=t["z_codes%d" % (n // 2)][:, jg, n % 2 * P : (n % 2 + 1) * P].bitcast(E4M3),
                        rhs_scale=z_sc[:, jg, cols],
                        start=(jg == 0),
                        stop=(jg == GROUPS - 1),
                    )

        def b_add(k):
            lg, n = divmod(k, 8)
            g, part = divmod(n, 4)
            name = "b_grp%d%d" % (lg, g)
            if part == 0:
                rotating("b_grp", name, [P, PACK, P, PACK], BF16, 2)
            nc.vector.tensor_tensor(
                out=t[name][:, :, 32 * part : 32 * (part + 1), :],
                in0=t["b_acc%d" % k][:].rearrange("p (tl m tc) -> p tc m tl", tl=PACK, tc=PACK),
                in1=t["h"][:, lg, :].unsqueeze(1).unsqueeze(1).broadcast_to([P, PACK, 32, PACK]),
                op=ADD,
            )

        def b_quantize(lg, g):
            codes = kept("b_codes%d%d" % (lg, g), [P, KP], U32)
            scales = kept("b_sc%d%d" % (lg, g), [P, KP], U8)
            quantize(codes[:], scales[:], t["b_grp%d%d" % (lg, g)][:].rearrange("p t m s -> p (t m s)"))

        def r_transposes(n, index):
            half, g, u = r_units[n]
            acc = bank("r_acc%d" % n, index)
            for i in range(4):
                if half == 1:
                    words = t["r_sorted%d" % g][:, i, u, :]
                else:
                    words = t["r_raw0"][:, i, :].bitcast(F32)[:, 256 * g + u : 256 * (g + 1) : 2]
                nc.tensor.transpose(acc[:, i * P : (i + 1) * P], words, ident[:])

        def r_sort(g):
            dst = rotating("raw", "r_sorted%d" % g, [P, 4, 2, P], F32, 8)
            words = t["r_raw1"][:, :, g * KP : (g + 1) * KP].bitcast(F32).rearrange("a i (p u) -> a i p u", u=2)
            nc.scalar.copy(out=dst[:].rearrange("a i u p -> a i p u"), in_=words)

        def r_scale(n):
            half, g, u = r_units[n]
            pairs = t["r_acc%d" % n][:].bitcast(BF16).rearrange("p (i m w) -> p m i w", i=4, w=2)
            for w in range(2):
                tc_ = 2 * u + w
                dst = kept("rps%d%d%d" % (half, g, tc_), [P, KP], F32)
                nc.scalar.activation(
                    out=dst[:].rearrange("p (m i) -> p m i", i=4),
                    in_=pairs[:, :, :, w],
                    func=COPY,
                    scale=t["ps"][:, g, tc_ : tc_ + 1],
                )

        def a_matmuls(s, banks):
            q, lg = a_steps[s]
            for i in range(AW // P):
                acc = bank("a_acc%d%d" % (s, i), banks[i])
                a0 = q * AW + i * P
                for bg in range(GROUPS):
                    nc.tensor.matmul_mx(
                        out=acc[:],
                        lhsT=f_codes[:, bg, 2 * a0 : 2 * (a0 + P)].bitcast(E2M1),
                        lhsT_scale=f_sc[:, bg, a0 : a0 + P],
                        rhs=t["x_codes%d%d" % (bg, lg)][:].bitcast(E4M3),
                        rhs_scale=t["x_sc%d%d" % (bg, lg)][:],
                        start=(bg == 0),
                        stop=(bg == GROUPS - 1),
                    )

        def a_add(s, i):
            q, lg = a_steps[s]
            dst = rotating("a_rows", "a_rows%d%d" % (s, i), [P, 2, P, 2], BF16, 6)
            nc.vector.tensor_tensor(
                out=dst[:],
                in0=t["a_acc%d%d" % (s, i)][:].rearrange("a (p u w) -> a u p w", u=2, w=2),
                in1=t["e_raw%d" % q][:, i, lg * KP : (lg + 1) * KP].rearrange("a (p u w) -> a u p w", u=2, w=2),
                op=ADD,
            )

        def a_transposes(s, index):
            acc = bank("a_turned%d" % s, index)
            for i in range(AW // P):
                words = t["a_rows%d%d" % (s, i)][:].rearrange("a u p w -> a (u p w)").bitcast(F32)
                for u in range(2):
                    col = u * AW + i * P
                    nc.tensor.transpose(acc[:, col : col + P], words[:, u * P : (u + 1) * P], ident[:])

        def a_copy(s):
            grp = rotating("a_grp", "a_grp%d" % s, [P, AW * PACK], BF16, 3)
            nc.scalar.copy(
                out=grp[:].bitcast(F32).rearrange("p (a u) -> p a u", u=2),
                in_=t["a_turned%d" % s][:].rearrange("p (u a) -> p a u", u=2),
            )

        def a_quantize(s):
            codes = kept("a_codes%d" % s, [P, AW], U32)
            scales = kept("a_sc%d" % s, [P, AW], U8)
            quantize(codes[:], scales[:], t["a_grp%d" % s][:])

        def g_matmuls(j, banks):
            a0, width, g = g_steps[j]
            q, within = divmod(a0, AW)
            cols = slice(within, within + width)
            for tc_ in range(PACK):
                n, place = divmod(tc_ * width, KP)
                if place == 0:
                    acc = bank("g_acc%d%d" % (j, n), banks[n])
                slot = slice(tc_ * P, (tc_ + 1) * P)
                for lg in range(GROUPS):
                    s = a_steps.index((q, lg))
                    nc.tensor.matmul_mx(
                        out=acc[:, place : place + width],
                        lhsT=t["b_codes%d%d" % (lg, g)][:, slot].bitcast(E4M3),
                        lhsT_scale=t["b_sc%d%d" % (lg, g)][:, slot],
                        rhs=t["a_codes%d" % s][:, cols].bitcast(E4M3),
                        rhs_scale=t["a_sc%d" % s][:, cols],
                        start=(lg == 0),
                        stop=(lg == GROUPS - 1),
                    )

        def y_finish(j, u):
            a0, width, g = g_steps[j]
            half, within = divmod(a0, KP)
            if u == 0 and a0 % AW == 0:
                rotating("y_t", "y_t%d%d" % (a0 // AW, g), [P, PACK, AW], F32, 3)
            cols = slice(a0 % AW, a0 % AW + width)
            for tc_ in (2 * u, 2 * u + 1):
                n, place = divmod(tc_ * width, KP)
                nc.vector.scalar_tensor_tensor(
                    out=t["y_t%d%d" % (a0 // AW, g)][:, tc_, cols],
                    in0=t["g_acc%d%d" % (j, n)][:, place : place + width],
                    scalar=t["step"][:, g, tc_ : tc_ + 1],
                    in1=t["rps%d%d%d" % (half, g, tc_)][:, within : within + width],
                    op0=MULT,
                    op1=ADD,
                )

        def y_group(j, engine, first, last):
            q, g = divmod(j, GROUPS)
            cols = slice(first * AW // 8, last * AW // 8)
            if "y_grp%d" % j not in t:
                rotating("y_grp", "y_grp%d" % j, [P, AW, PACK], BF16, 3)
            copy_on(
                engine,
                t["y_grp%d" % j][:, cols, :].rearrange("p (c i) s -> p c s i", i=4),
                t["y_t%d%d" % (q, g)][:, :, cols].rearrange("p s (c i) -> p c s i", i=4),
            )

        y_sc = kept("y_sc", [P, GROUPS, SIZE], U8)
        y_codes = [kept("y_codes%d" % g, [P, SIZE], U32) for g in range(GROUPS)]

        def y_quantize(j):
            q, g = divmod(j, GROUPS)
            cols = slice(q * AW, (q + 1) * AW)
            quantize(y_codes[g][:, cols], y_sc[:, g, cols], t["y_grp%d" % j][:].rearrange("p a s -> p (a s)"))

        def y_store_codes(j):
            a0, g = g_steps[j][0], g_steps[j][2]
            cols = slice(a0, a0 + AW)
            nc.sync.dma_start(
                out=out_1[g, :, cols, :].rearrange("p a s -> p (a s)").bitcast(I32),
                in_=y_codes[g][:, cols].bitcast(I32),
            )

        def y_transposes(j, banks):
            a0, width, g = g_steps[j]
            for i in range(width // P):
                acc = bank("y_turned%d%d" % (j, i), banks[i])
                cols = slice(a0 % AW + i * P, a0 % AW + (i + 1) * P)
                for tc_ in range(PACK):
                    nc.tensor.transpose(
                        acc[:, tc_ * P : (tc_ + 1) * P], t["y_t%d%d" % (a0 // AW, g)][:, tc_, cols], ident[:]
                    )

        def y_store(j):
            a0, width, g = g_steps[j]
            for i in range(width // P):
                rows = rotating("y_rows", "y_rows%d%d" % (j, i), [P, P, PACK], F32, 6)
                nc.scalar.copy(out=rows[:], in_=t["y_turned%d%d" % (j, i)][:].rearrange("a (s p) -> a p s", s=PACK))
                nc.sync.dma_start(
                    out=out_0[a0 + i * P : a0 + (i + 1) * P, g * KP : (g + 1) * KP],
                    in_=rows[:].rearrange("a p s -> a (p s)"),
                )

        S, V = nc.scalar, nc.vector
        r_units = [(half, g, u) for half in range(2) for g in range(GROUPS) for u in range(2)]
        a_steps = [(0, 0), (1, 0), (0, 1), (1, 1), (2, 0), (2, 1), (3, 0), (3, 1)]
        g_steps = [(q * AW, AW, g) for q in range(SIZE // AW) for g in range(GROUPS)][:-1]
        g_steps.extend([(SIZE - 2 * P, P, 1), (SIZE - P, P, 1)])
        both = [(V, slice(0, 3)), (S, slice(3, 4))]
        group_d(0, 0, both)
        quantize_input("d", 0, 0)
        group_d(1, 0, [(S, slice(2, 4)), (V, slice(0, 2))])
        quantize_input("d", 1, 0)
        group_d(0, 1, both)
        group_d(1, 1, [(S, slice(0, 4))])
        group_x(0, 0, S)
        for k in range(4):
            b_matmuls(k, k)
        for k in range(12):
            if k == 1:
                quantize_input("d", 0, 1)
                group_x(1, 0, S)
            if k == 4:
                quantize_input("d", 1, 1)
                group_x(0, 1, S)
            if k == 8:
                quantize_input("x", 0, 0)
                group_x(1, 1, S)
            if k == 11:
                quantize_input("x", 1, 0)
            b_add(k)
            if k + 4 < 14:
                b_matmuls(k + 4, k % 4)
            if k == 9:
                r_transposes(0, 4)
                r_transposes(1, 5)
            if k % 4 == 1 and k > 1:
                b_quantize(*divmod(k // 4 - 1, GROUPS))
        ps = kept("ps", [P, GROUPS, PACK], F32)
        nc.vector.tensor_tensor(out=ps[:], in0=t["penalty"][:], in1=t["step"][:], op=MULT)

        a_matmuls(0, (2, 3))
        b_add(12)
        quantize_input("x", 0, 1)
        b_add(13)
        b_quantize(1, 0)
        a_matmuls(1, (0, 1))
        r_scale(0)
        r_scale(1)
        a_add(0, 0)
        a_add(0, 1)
        quantize_input("x", 1, 1)
        r_transposes(2, 6)
        a_transposes(0, 4)
        a_matmuls(2, (2, 3))
        a_add(1, 0)
        a_add(1, 1)
        a_copy(0)
        r_scale(2)
        b_matmuls(14, 0)
        a_add(2, 0)
        a_add(2, 1)
        r_transposes(3, 7)
        a_transposes(1, 4)
        a_transposes(2, 5)
        a_copy(2)
        a_copy(1)
        b_matmuls(15, 1)
        a_matmuls(3, (2, 3))
        a_quantize(0)
        b_add(14)
        a_quantize(2)
        b_add(15)
        r_scale(3)
        r_sort(0)
        r_sort(1)
        a_add(3, 0)
        a_quantize(1)
        a_add(3, 1)

        steps = len(g_steps)
        for j in range(steps):
            s = j + 4
            if 1 <= j < steps - 1:
                y_group(j - 1, S, 5, 8)
            g_matmuls(j, (0, 1) if j >= 4 and j % 2 == 1 else (4, 5))
            if s < len(a_steps):
                a_matmuls(s, (0, 1))
            if s - 1 < len(a_steps):
                a_transposes(s - 1, 2)
                a_copy(s - 1)
            if 1 <= j:
                y_transposes(j - 1, (2, 7) if j >= 5 and j % 2 == 1 else (3, 6))
                y_store(j - 1)
            if s < len(r_units):
                r_transposes(s, 7)
                r_scale(s)
            y_finish(j, 0)
            if j == 0:
                b_quantize(1, 1)
            if 3 <= s - 2 < len(a_steps):
                a_quantize(s - 2)
            if 2 <= j < steps - 1:
                y_quantize(j - 2)
                y_store_codes(j - 2)
            y_finish(j, 1)
            if 1 <= j < steps - 1:
                y_group(j - 1, V, 0, 5)
            if s < len(a_steps):
                a_add(s, 0)
                a_add(s, 1)
        y_quantize(steps - 3)
        y_store_codes(steps - 3)
        y_group(steps - 2, V, 0, 8)
        y_transposes(steps - 1, (2, 7))
        y_quantize(steps - 2)
        y_store(steps - 1)
        y_store_codes(steps - 2)

        for quad in range(4):
            nc.sync.dma_start(
                out=out_2[:, 4 * quad : 4 * quad + 4, :].rearrange("g r n -> r g n").bitcast(I32),
                in_=y_sc[32 * quad : 32 * quad + 4, :, :].bitcast(I32),
            )
